import numpy as np
import ml_dtypes


def mxq(x, axis, fmt="e4m3"):
    dtype, down = {"e4m3": (ml_dtypes.float8_e4m3fn, 7), "e5m2": (ml_dtypes.float8_e5m2, 14)}[fmt]
    v = np.moveaxis(np.asarray(x, np.float32).astype(ml_dtypes.bfloat16).astype(np.float64), axis, -1)
    blocks = v.reshape(v.shape[:-1] + (-1, 32))
    amax = np.abs(blocks).max(-1, keepdims=True)
    byte = np.maximum(np.where(amax > 0, np.frexp(amax)[1] - 1 + 127, 0) - down, 1)
    scale = np.exp2(byte - 127.0)
    codes = (blocks / scale).astype(np.float32).astype(dtype).astype(np.float64)
    return np.moveaxis((codes * scale).reshape(v.shape), -1, axis)


WIDE = False


def mx_kscale(k):
    if not WIDE:
        return np.ones(k)
    levels = np.array([10, -10, 5, -5, 0])
    if k % 512:
        return np.exp2(np.random.permutation(np.resize(levels, k // 32))).repeat(32)
    a = np.empty((k // 512, 16))
    for p in range(k // 512):
        a[p, :8] = np.random.permutation(np.resize(levels, 8))
        for g in range(8):
            far = levels[np.abs(levels - a[p, g]) >= 10]
            a[p, g + 8] = far[np.random.randint(len(far))]
    return np.exp2(a.ravel()).repeat(32)


def f64(x):
    return np.asarray(x).astype(np.float64)


def striped(idx):
    return np.tile(idx.reshape(-1, 16).T, (8, 1)).astype(np.uint16)


def unstriped(offs):
    return offs[:16].T.reshape(-1).astype(np.int64)


def striped8(idx):
    return np.concatenate([x.reshape(-1, 16).T for x in idx]).astype(np.uint16)


def runs(offs, k):
    lists = np.stack([offs[16 * r : 16 * r + 16].T.reshape(-1) for r in range(8)]).astype(np.int64)
    return lists[np.arange(k) % 512 // 64]


def pack_weight(w):
    k, n = w.shape
    w = f64(np.asarray(w, np.float32).astype(ml_dtypes.bfloat16)).reshape(k // 32, 32, n)
    amax = np.abs(w).max(1)
    byte = np.clip(np.where(amax > 0, np.frexp(amax)[1] - 1 + 127 - 7, 1), 1, 254)
    scaled = (w * np.exp2(127.0 - byte)[:, None, :]).reshape(k, n).astype(np.float32)
    words = np.ascontiguousarray(scaled.reshape(k // 512, 128, 4, n).transpose(0, 1, 3, 2)).astype(ml_dtypes.float8_e4m3fn).view(np.uint8)
    return words, np.ascontiguousarray(byte.astype(np.uint8).reshape(k // 512, 16, n))


def unpack_weight(words, scales):
    g, p, n, _ = words.shape
    vals = np.ascontiguousarray(words).view(ml_dtypes.float8_e4m3fn).astype(np.float64) * np.repeat(np.exp2(scales.astype(np.float64) - 127.0), 8, axis=1)[..., None]
    return vals.transpose(0, 1, 3, 2).reshape(g * 512, n)


K, T, S, H, W, G, U = 512, 1024, 256, 512, 128, 2048, 1024


def setup_inputs():
    n = np.random.standard_normal
    s = mx_kscale(K)[:, None]
    packed_xT = pack_weight(n((K, T)) * s)
    packed_w1 = pack_weight(n((K, H)) / np.sqrt(2 * K) / s)
    packed_w2 = pack_weight(n((K, H)) / np.sqrt(2 * K) / s)
    packed_dT = pack_weight(n((K, G)) / s)
    return {
        "x_words": packed_xT[0],
        "x_scales": packed_xT[1],
        "w1_words": packed_w1[0],
        "w1_scales": packed_w1[1],
        "w2_words": packed_w2[0],
        "w2_scales": packed_w2[1],
        "gs": (np.random.uniform(0.5, 1.5, (K, 1)) * s).astype(np.float32),
        "d_words": packed_dT[0],
        "d_scales": packed_dT[1],
        "mem": n((H, U)).astype(np.float32),
        "offs": striped(np.random.permutation(T)[:S]),
        "hz": striped8(np.random.randint(0, T, (8, S))),
        "n1": striped(np.random.permutation(S)[:W]),
        "n2": striped(np.random.permutation(S)[:W]),
        "n3": striped(np.random.permutation(S)),
        "k1": striped8(np.random.randint(0, G, (8, H))),
        "n4": striped(np.random.permutation(U)[:S]),
    }


def reference(x_words, x_scales, w1_words, w1_scales, w2_words, w2_scales, gs, d_words, d_scales, mem, offs, hz, n1, n2, n3, k1, n4):
    d_k1 = unpack_weight(d_words, d_scales)[np.arange(K)[:, None], runs(k1, K)]
    xq = unpack_weight(x_words, x_scales)[:, unstriped(offs)]
    x_hz = unpack_weight(x_words, x_scales)[np.arange(K)[:, None], runs(hz, K)]
    y = unpack_weight(w1_words, w1_scales).T @ xq + unpack_weight(w2_words, w2_scales).T @ x_hz
    pa = y[:, unstriped(n2)]
    ds = y.copy()
    ds[:, unstriped(n1)] = pa
    z = f64(gs) * (ds - (0.5 * ds[:, unstriped(n3)]))
    h = 0.0625 * ((d_k1.T @ mxq(z, 0, "e4m3")))
    nw = np.maximum(h, 0.5 * f64(mem)[:, unstriped(n4)])
    out = f64(mem).copy()
    out[:, unstriped(n4)] = nw
    return out

from contextlib import ExitStack

import concourse.mybir as mybir

F32 = mybir.dt.float32
BF16 = mybir.dt.bfloat16
I32 = mybir.dt.int32
U32 = mybir.dt.uint32
U16 = mybir.dt.uint16
U8 = mybir.dt.uint8
FP8X4 = mybir.dt.float8_e4m3fn_x4
COPY = mybir.ActivationFunctionType.Copy
MULT = mybir.AluOpType.mult
ADD = mybir.AluOpType.add
MAX = mybir.AluOpType.max

K, T, S, H, W, G, U = 512, 1024, 256, 512, 128, 2048, 1024
P = 128
PACK = 4
HALF = S // 2
FLOPS = 3 * 2 * K * H * S


def words_of(packed):
    return packed[0].rearrange("p n t -> p (n t)").bitcast(I32)


def rows_times_8(scales):
    rows = scales[0].bitcast(I32)
    return rows.unsqueeze(1).to_broadcast([16, 8, rows.shape[1]])


def place_rows(nc, placed, spread):
    for r in range(1, 4):
        nc.sync.dma_start(placed.bitcast(I32)[r:P:32, :], spread.bitcast(I32)[8 * r : P : 32, :])


def tile_picked_thqksetpagex_none_p_kernel(
    tc, x_words, x_scales, w1_words, w1_scales, w2_words, w2_scales, gs, d_words, d_scales, mem, offs, hz, n1, n2, n3, k1, n4, out
):
    nc = tc.nc
    with ExitStack() as ctx:
        lists = ctx.enter_context(tc.tile_pool(name="lists", bufs=1))
        sb = ctx.enter_context(tc.tile_pool(name="sb", bufs=1))
        psum = ctx.enter_context(tc.psum_pool(name="psum", bufs=1))

        def load_list(source, name):
            held = lists.tile(list(source.shape), U16, name=name)
            nc.sync.dma_start(held[:], source)
            return held

        x_bytes = sb.tile([P, T], U8, name="x_bytes", align_bytes=64)
        w_bytes = sb.tile([P, 2 * H], U8, name="w_bytes", align_bytes=64)
        d_bytes = sb.tile([P, G], U8, name="d_bytes", align_bytes=64)
        nc.vector.memset(d_bytes[:].bitcast(I32), 0)

        nc.scalar.dma_start(x_bytes[:].bitcast(I32), rows_times_8(x_scales))
        hz_l = load_list(hz, "hz_l")
        offs_l = load_list(offs, "offs_l")
        x_table = sb.tile([P, T], U32, name="x_table", tag="x_then_d", align_bytes=64)
        nc.sync.dma_start(x_table[:].bitcast(I32), words_of(x_words))
        for a, scales in enumerate((w1_scales, w2_scales)):
            nc.scalar.dma_start(w_bytes[:, a * H : (a + 1) * H].bitcast(I32), rows_times_8(scales))
        w1_raw = sb.tile([P, H], U32, name="w1_raw", tag="slot0", align_bytes=64)
        w2_raw = sb.tile([P, H], U32, name="w2_raw", tag="slot1", align_bytes=64)
        nc.sync.dma_start(w1_raw[:].bitcast(I32), words_of(w1_words))
        nc.sync.dma_start(w2_raw[:].bitcast(I32), words_of(w2_words))
        n2_l = load_list(n2, "n2_l")
        n1_l = load_list(n1, "n1_l")
        n3_l = load_list(n3, "n3_l")
        n4_l = load_list(n4, "n4_l")
        k1_l = load_list(k1, "k1_l")
        gain = sb.tile([P, PACK], F32, name="gain")
        nc.gpsimd.dma_start(gain[:], gs.rearrange("(p t) o -> p (t o)", t=PACK))
        nc.gpsimd.dma_start(d_bytes[:].bitcast(I32)[0:P:8, :], d_scales[0].bitcast(I32))

        x_picked = sb.tile([P, 2 * S], U8, name="x_picked", align_bytes=64)
        nc.vector.tensor_copy(x_picked[:, S:], x_bytes[:].indirect(hz_l[:]))
        nc.vector.tensor_copy(x_picked[:, :S], x_bytes[:].indirect(offs_l[:]))
        planes = sb.tile([P, 2 * S + 2 * H], U8, name="planes", align_bytes=64)
        x_plane = planes[:, : 2 * S]
        w_plane = planes[:, 2 * S :]
        nc.vector.tensor_copy(x_plane.bitcast(I32), x_picked[:].bitcast(I32))
        nc.vector.tensor_copy(
            w_plane.rearrange("p (a t m) -> p a t m", a=2, t=PACK),
            w_bytes[:].rearrange("p (a m t) -> p a t m", a=2, t=PACK),
        )
        place_rows(nc, planes[:], planes[:])

        x_codes = []
        for name, tag, picks in (("x_offs", "slot2", offs_l), ("x_hz", "slot3", hz_l)):
            codes = sb.tile([P, S], U32, name=name, tag=tag, align_bytes=64)
            nc.vector.tensor_copy(codes[:], x_table[:].indirect(picks[:]))
            x_codes.append(codes)
        w_codes = []
        for name, raw in (("w1_codes", w1_raw), ("w2_codes", w2_raw)):
            codes = sb.tile([P, H], U32, name=name, align_bytes=64)
            nc.scalar.copy(
                codes[:].rearrange("p (t m) -> p m t", t=PACK),
                raw[:].rearrange("p (m t) -> p m t", t=PACK),
            )
            w_codes.append(codes)

        d_table = sb.tile([P, G], U32, name="d_table", tag="x_then_d", align_bytes=64)
        nc.sync.dma_start(d_table[:].bitcast(I32), words_of(d_words))
        def fetch_old(t):
            held = sb.tile([P, S], F32, name=f"old{t}")
            nc.scalar.activation(held[:], pages[t][:].indirect(n4_l[:]), COPY, scale=0.5)
            return held


        rows = []
        for t in range(PACK):
            y = psum.tile([P, S], F32, name=f"y{t}", tag=f"bank{t}")
            for a in range(2):
                nc.tensor.matmul_mx(
                    out=y[:],
                    lhsT=w_codes[a][:, t * P : (t + 1) * P].bitcast(FP8X4),
                    lhsT_scale=w_plane[:, a * H + t * P : a * H + (t + 1) * P],
                    rhs=x_codes[a][:].bitcast(FP8X4),
                    rhs_scale=x_plane[:, a * S : (a + 1) * S],
                    start=(a == 0),
                    stop=(a == 1),
                )
            row = sb.tile([P, S], F32, name=f"row{t}")
            nc.vector.tensor_scalar(row[:], y[:], gain[:, t : t + 1], None, MULT)
            rows.append(row)

        pages = []
        for t in range(PACK):
            page = sb.tile([P, U], F32, name=f"page{t}", tag=f"slot{t}", align_bytes=64)
            nc.sync.dma_start(page[:], mem[t * P : (t + 1) * P, :])
            pages.append(page)

        z = [sb.tile([P, HALF, PACK], BF16, name=f"z{h}", align_bytes=64) for h in range(2)]

        def mix(h, t, fetched):
            nc.scalar.activation(fetched, rows[t][:].indirect(n3_l[:, 8 * h : 8 * (h + 1)]), COPY)
            nc.vector.scalar_tensor_tensor(z[h][:, :, t], fetched, -0.5, rows[t][:, h * HALF : (h + 1) * HALF], MULT, ADD)

        for t in range(PACK):
            pa = sb.tile([P, W], F32, name=f"pa{t}", tag=f"pa{t}")
            nc.scalar.activation(pa[:], rows[t][:].indirect(n2_l[:]), COPY)
            nc.scalar.activation(rows[t][:].indirect(n1_l[:]), pa[:], COPY)
            first = sb.tile([P, HALF], F32, name=f"first{t}")
            mix(0, t, first[:])

        d_picked = sb.tile([P, H], U8, name="d_picked", align_bytes=64)
        nc.vector.tensor_copy(d_picked[:], d_bytes[:].indirect(k1_l[:]))
        d_plane = sb.tile([P, H], U8, name="d_plane", align_bytes=64)
        nc.vector.tensor_copy(d_plane[:].bitcast(I32), d_picked[:].bitcast(I32))
        place_rows(nc, d_plane[:], d_picked[:])
        d_codes = sb.tile([P, H], U32, name="d_codes", align_bytes=64)
        nc.vector.tensor_copy(d_codes[:], d_table[:].indirect(k1_l[:]))

        new = [sb.tile([P, S], F32, name=f"new{t}") for t in range(PACK)]

        def second_product(h):
            z_codes = sb.tile([P, HALF], U32, name=f"z_codes{h}", align_bytes=64)
            z_plane = sb.tile([P, HALF], U8, name=f"z_plane{h}", align_bytes=64)
            nc.vector.quantize_mx(out=z_codes[:].bitcast(FP8X4), scales=z_plane[:], in_=z[h][:].rearrange("p c t -> p (c t)"))
            for t in range(PACK):
                hsum = psum.tile([P, HALF], F32, name=f"h{h}{t}", tag=f"bank{PACK * (1 - h) + t}")
                nc.tensor.matmul_mx(
                    out=hsum[:],
                    lhsT=d_codes[:, t * P : (t + 1) * P].bitcast(FP8X4),
                    lhsT_scale=d_plane[:, t * P : (t + 1) * P],
                    rhs=z_codes[:].bitcast(FP8X4),
                    rhs_scale=z_plane[:],
                    start=True,
                    stop=True,
                )
                cols = slice(h * HALF, (h + 1) * HALF)
                nc.vector.scalar_tensor_tensor(new[t][:, cols], hsum[:], 0.0625, old[t][:, cols], MULT, MAX)

        second = sb.tile([P, PACK, HALF], F32, name="second", tag=f"pa{PACK - 1}")
        for t in range(PACK):
            mix(1, t, second[:, t, :])
        old = [fetch_old(t) for t in range(PACK)]
        second_product(0)
        second_product(1)

        for h in range(2):
            for t in range(2):
                nc.scalar.activation(pages[t][:].indirect(n4_l[:, 8 * h : 8 * (h + 1)]), new[t][:, h * HALF : (h + 1) * HALF], COPY)
        for t in range(2, PACK):
            nc.scalar.activation(pages[t][:].indirect(n4_l[:]), new[t][:], COPY)
        for t in range(PACK):
            nc.sync.dma_start(out[t * P : (t + 1) * P, :], pages[t][:])
